import numpy as np
import ml_dtypes


def mxq(x, axis, fmt="e4m3"):
    dtype, down = {"e4m3": (ml_dtypes.float8_e4m3fn, 7), "e5m2": (ml_dtypes.float8_e5m2, 14)}[fmt]
    v = np.moveaxis(np.asarray(x, np.float32).astype(ml_dtypes.bfloat16).astype(np.float64), axis, -1)
    blocks = v.reshape(v.shape[:-1] + (-1, 32))
    amax = np.abs(blocks).max(-1, keepdims=True)
    byte = np.maximum(np.where(amax > 0, np.frexp(amax)[1] - 1 + 127, 0) - down, 1)
    scale = np.exp2(byte - 127.0)
    codes = (blocks / scale).astype(np.float32).astype(dtype).astype(np.float64)
    return np.moveaxis((codes * scale).reshape(v.shape), -1, axis)


WIDE = False


def mx_kscale(k):
    if not WIDE:
        return np.ones(k)
    levels = np.array([30, -30])
    if k % 512:
        return np.exp2(np.random.permutation(np.resize(levels, k // 32))).repeat(32)
    a = np.empty((k // 512, 16))
    for p in range(k // 512):
        a[p, :8] = np.random.permutation(np.resize(levels, 8))
        for g in range(8):
            far = levels[np.abs(levels - a[p, g]) >= 10]
            a[p, g + 8] = far[np.random.randint(len(far))]
    return np.exp2(a.ravel()).repeat(32)


def f64(x):
    return np.asarray(x).astype(np.float64)


E2M1 = np.array([0.0, 0.5, 1.0, 1.5, 2.0, 3.0, 4.0, 6.0, -0.0, -0.5, -1.0, -1.5, -2.0, -3.0, -4.0, -6.0])


def pack_weight(w, fmt):
    k, n = w.shape
    w = f64(np.asarray(w, np.float32).astype(ml_dtypes.bfloat16)).reshape(k // 32, 32, n)
    amax = np.abs(w).max(1)
    if fmt == "e4m3":
        byte = np.frexp(amax)[1] - 1 + 127 - 7
    else:
        mant, ex = np.frexp(amax / 6.0)
        byte = np.where(mant > 0.5, ex, ex - 1) + 127
    byte = np.clip(np.where(amax > 0, byte, 1), 1, 254)
    scaled = (w * np.exp2(127.0 - byte)[:, None, :]).reshape(k, n).astype(np.float32)
    by_word = np.ascontiguousarray(scaled.reshape(k // 512, 128, 4, n).transpose(0, 1, 3, 2))
    if fmt == "e4m3":
        words = by_word.astype(ml_dtypes.float8_e4m3fn).view(np.uint8)
    else:
        c = by_word.astype(ml_dtypes.float4_e2m1fn).view(np.uint8) & 0xF
        words = (c[..., 0::2] | (c[..., 1::2] << 4)).reshape(k // 512, 128, 2 * n)
    return np.ascontiguousarray(words), np.ascontiguousarray(byte.astype(np.uint8).reshape(k // 512, 16, n))


def unpack_weight(words, scales, fmt):
    g, _, n = scales.shape
    words = np.ascontiguousarray(words).reshape(g, 128, n, -1)
    if fmt == "e4m3":
        vals = words.view(ml_dtypes.float8_e4m3fn).astype(np.float64)
    else:
        nib = np.empty((g, 128, n, 4), np.uint8)
        nib[..., 0::2] = words & 0xF
        nib[..., 1::2] = words >> 4
        vals = E2M1[nib]
    vals = vals * np.repeat(np.exp2(scales.astype(np.float64) - 127.0), 8, axis=1)[..., None]
    return vals.transpose(0, 1, 3, 2).reshape(g * 512, n)


def bf(x):
    return np.asarray(x, np.float32).astype(ml_dtypes.bfloat16)


def planes(Y):
    r, m = Y.shape
    b = f64(bf(Y)).reshape(r // 32, 32, m)
    amax = np.abs(b).max(1)
    byte = np.clip(np.where(amax > 0, np.frexp(amax)[1] - 1 + 127 - 7, 1), 1, 254)
    codes = (b * np.exp2(127.0 - byte)[:, None, :]).reshape(r, m).astype(np.float32).astype(ml_dtypes.float8_e4m3fn).view(np.uint8)
    words = codes.reshape(r // 512, 128, 4, m).transpose(0, 1, 3, 2)
    return np.ascontiguousarray(words), np.ascontiguousarray(byte.astype(np.uint8).reshape(r // 512, 16, m))


K, T, N = 1024, 512, 512


def setup_inputs():
    n = np.random.standard_normal
    fk = mx_kscale(K)
    wap = pack_weight(n((K, N)) * 1 / np.sqrt(K) * fk[:, None], "e4m3")
    wbp = pack_weight(n((K, N)) * 1 / np.sqrt(K) * fk[:, None], "e2m1")
    return {
        "xf": (n((K, T)) * 1.2).astype(np.float32),
        "lo": (np.random.uniform(-1.0, -0.4, (K, 1))).astype(np.float32),
        "hi": (np.random.uniform(0.4, 1.0, (K, 1))).astype(np.float32),
        "fa": (np.random.uniform(0.5, 2.0, (K, 1)) / fk[:, None]).astype(np.float32),
        "fb": (np.random.uniform(0.5, 2.0, (K, 1)) / fk[:, None]).astype(np.float32),
        "wa_words": wap[0],
        "wa_scales": wap[1],
        "wb_words": wbp[0],
        "wb_scales": wbp[1],
    }


def reference(xf, lo, hi, fa, fb, wa_words, wa_scales, wb_words, wb_scales):
    wau = unpack_weight(wa_words, wa_scales, "e4m3")
    wbu = unpack_weight(wb_words, wb_scales, "e2m1")
    b = np.maximum(np.minimum(f64(xf), f64(hi)), f64(lo))
    xa = b * f64(fa)
    xc = (f64(xf) - b) * f64(fb)
    xaq = mxq(xa, 0, "e4m3")
    xcq = mxq(xc, 0, "e5m2")
    y = wau.T @ xaq + wbu.T @ xcq
    words, scales = planes(y)
    return y, words, scales

@@ -1,0 +1,180 @@
+from contextlib import ExitStack
+
+import concourse.mybir as mybir
+
+K, T, N = 1024, 512, 512
+FLOPS = 2 * 2 * K * T * N
+
+F32 = mybir.dt.float32
+BF16 = mybir.dt.bfloat16
+I32 = mybir.dt.int32
+U8 = mybir.dt.uint8
+E4M3 = mybir.dt.float8_e4m3fn_x4
+E5M2 = mybir.dt.float8_e5m2_x4
+E2M1 = mybir.dt.float4_e2m1fn_x4
+ALU = mybir.AluOpType
+COPY = mybir.ActivationFunctionType.Copy
+
+P = 128
+PACK = 4
+PASSES = K // (P * PACK)
+HALF = T // 2
+WA_ROW = 4
+
+
+def tile_mix_kept_and_cut_off_pl_kernel(tc, xf, lo, hi, fa, fb, wa_words, wa_scales, wb_words, wb_scales, out_0, out_1, out_2):
+    nc = tc.nc
+    with ExitStack() as ctx:
+        sb = ctx.enter_context(tc.tile_pool(name="sb", bufs=1))
+        psum = ctx.enter_context(tc.psum_pool(name="psum", bufs=1))
+        ctx.enter_context(tc.manual_schedule())
+
+        def tile(name, shape, dtype):
+            return sb.tile(shape, dtype, name=name, align_bytes=64)
+
+        slots = [(z, j) for z in range(PASSES) for j in range(PACK)]
+        x = {s: tile("x%d%d" % s, [P, T], F32) for s in slots}
+        b = {s: tile("b%d%d" % s, [P, T], F32) for s in slots}
+        d = {s: tile("d%d%d" % s, [P, T], F32) for s in slots}
+        par = {n: tile(n, [P, PASSES, PACK], F32) for n in ("hi", "lo", "fa", "fb")}
+        ops = [(o, z) for o in ("a", "c") for z in range(PASSES)]
+        rows = {s: tile("rows%s%d" % s, [P, PACK, T], BF16) for s in ops}
+        grouped = {(o, z, h): tile("grp%s%d%d" % (o, z, h), [P, HALF * PACK], BF16) for o, z in ops for h in range(2)}
+        codes = {s: tile("codes%s%d" % s, [P, T], I32) for s in ops}
+        scales = {s: tile("scales%s%d" % s, [P, T], U8) for s in ops}
+        wa_raw = tile("wa_raw", [P, PASSES * N], I32)
+        wb_raw = tile("wb_raw", [P, PASSES * 2 * N], U8)
+        ws_raw = tile("ws_raw", [P, PASSES * N], U8)
+        wa = tile("wa", [P, PASSES * N], I32)
+        wb = tile("wb", [P, PASSES * 2 * N], U8)
+        ws = tile("ws", [P, PASSES * N], U8)
+        acc = [psum.tile([P, T], F32, name="acc%d" % r) for r in range(PACK)]
+        y = [tile("y%d" % h, [P, PACK, HALF], F32) for h in range(2)]
+        y_grouped = [tile("yg%d" % h, [P, HALF * PACK], BF16) for h in range(2)]
+        y_codes = [tile("yc%d" % h, [P, HALF], I32) for h in range(2)]
+        y_scales = tile("ys", [P, T], U8)
+
+        nc.vector.memset(ws_raw[:].bitcast(I32), 0)
+
+        for name, src in (("hi", hi), ("lo", lo), ("fa", fa), ("fb", fb)):
+            nc.scalar.dma_start(out=par[name][:], in_=src.rearrange("(z p j) o -> p z (j o)", p=P, j=PACK))
+        x_rows = xf.rearrange("(z p j) t -> z j p t", p=P, j=PACK)
+        for z, j in slots:
+            nc.sync.dma_start(out=x[z, j][:], in_=x_rows[z, j])
+        nc.sync.dma_start(out=wa_raw[:].rearrange("p (z c) -> p z c", z=PASSES), in_=wa_words.rearrange("z p c r -> p z (c r)").bitcast(I32))
+        ws_words = ws_raw[:].bitcast(I32).rearrange("p (z c) -> p z c", z=PASSES)
+        for row0, src in ((WA_ROW, wa_scales), (0, wb_scales)):
+            for q in range(4):
+                nc.sync.dma_start(
+                    out=ws_words[32 * q + row0 : 32 * q + row0 + 4],
+                    in_=src[:, 4 * q : 4 * q + 4, :].rearrange("z r c -> r z c").bitcast(I32),
+                )
+        nc.sync.dma_start(out=wb_raw[:].bitcast(I32).rearrange("p (z c) -> p z c", z=PASSES), in_=wb_words.rearrange("z p c -> p z c").bitcast(I32))
+
+        def col(name, z, j):
+            return par[name][:, z, j : j + 1]
+
+        def clamp(z, j):
+            nc.vector.tensor_scalar(out=b[z, j][:], in0=x[z, j][:], scalar1=col("hi", z, j), scalar2=col("lo", z, j), op0=ALU.min, op1=ALU.max)
+
+        def cut(z, j):
+            nc.vector.tensor_tensor(out=d[z, j][:], in0=x[z, j][:], in1=b[z, j][:], op=ALU.subtract)
+
+        def scale_rows(o, z):
+            src, factor = (b, "fa") if o == "a" else (d, "fb")
+            for j in range(PACK):
+                nc.scalar.activation(out=rows[o, z][:, j, :], in_=src[z, j][:], func=COPY, scale=col(factor, z, j))
+
+        def interleave(engine, dst, src):
+            out = dst.rearrange("p (c i j) -> p c j i", i=4, j=PACK)
+            in_ = src.rearrange("p j (c i) -> p c j i", i=4)
+            if engine == "vector":
+                nc.vector.tensor_copy(out=out, in_=in_)
+            else:
+                nc.scalar.copy(out=out, in_=in_)
+
+        def group(engine, o, z, h):
+            interleave(engine, grouped[o, z, h][:], rows[o, z][:, :, h * HALF : (h + 1) * HALF])
+
+        def quantize(o, z, h):
+            cols = slice(h * HALF, (h + 1) * HALF)
+            nc.vector.quantize_mx(out=codes[o, z][:, cols].bitcast(E4M3 if o == "a" else E5M2), scales=scales[o, z][:, cols], in_=grouped[o, z, h][:])
+
+        def deal_wa():
+            nc.vector.tensor_copy(out=wa[:].rearrange("p (r c i) -> p c r i", r=PACK, i=4), in_=wa_raw[:].rearrange("p (c i r) -> p c r i", r=PACK, i=4))
+
+        def deal_wb():
+            nc.vector.tensor_copy(out=wb[:].rearrange("p (r m e) -> p r m e", r=PACK, e=2), in_=wb_raw[:].rearrange("p (m r e) -> p r m e", r=PACK, e=2))
+
+        def deal_scales():
+            nc.vector.tensor_copy(out=ws[:].rearrange("p (r m) -> p r m", r=PACK), in_=ws_raw[:].rearrange("p (m r) -> p r m", r=PACK))
+
+        def multiply(o, z, start=False, stop=False):
+            for r in range(PACK):
+                c0 = (r * PASSES + z) * P
+                if o == "a":
+                    lhs, lhs_scale, fmt = wa[:, c0 : c0 + P].bitcast(E4M3), ws[WA_ROW:P, c0 : c0 + P], E4M3
+                else:
+                    lhs, lhs_scale, fmt = wb[:, 2 * c0 : 2 * c0 + 2 * P].bitcast(E2M1), ws[:, c0 : c0 + P], E5M2
+                nc.tensor.matmul_mx(out=acc[r][:], lhsT=lhs, lhsT_scale=lhs_scale, rhs=codes[o, z][:].bitcast(fmt), rhs_scale=scales[o, z][:], start=start, stop=stop)
+
+        clamp(*slots[0])
+        for prev, cur in zip(slots[:-2], slots[1:-1]):
+            clamp(*cur)
+            cut(*prev)
+        clamp(*slots[-1])
+        cut(*slots[-2])
+        scale_rows("a", 0)
+        scale_rows("c", 0)
+        group("scalar", "a", 0, 0)
+        group("scalar", "a", 0, 1)
+        deal_wa()
+        cut(*slots[-1])
+        scale_rows("c", 1)
+        scale_rows("a", 1)
+        group("scalar", "a", 1, 1)
+        deal_scales()
+        quantize("a", 0, 0)
+        quantize("a", 0, 1)
+        multiply("a", 0, start=True)
+        group("vector", "c", 0, 0)
+        group("vector", "c", 0, 1)
+        deal_wb()
+        quantize("c", 0, 0)
+        quantize("c", 0, 1)
+        multiply("c", 0)
+        group("vector", "c", 1, 0)
+        group("vector", "c", 1, 1)
+        quantize("c", 1, 0)
+        quantize("c", 1, 1)
+        multiply("c", 1)
+        group("vector", "a", 1, 0)
+        quantize("a", 1, 1)
+        quantize("a", 1, 0)
+        multiply("a", 1, stop=True)
+
+        out_rows = out_0.rearrange("(p r) t -> p r t", r=PACK)
+        out_words = out_1.rearrange("z p c r -> p (z c r)").bitcast(I32)
+
+        def finish(h):
+            cols = slice(h * HALF, (h + 1) * HALF)
+            interleave("vector", y_grouped[h][:], y[h][:])
+            nc.vector.quantize_mx(out=y_codes[h][:].bitcast(E4M3), scales=y_scales[:, cols], in_=y_grouped[h][:])
+            nc.sync.dma_start(out=out_words[:, cols], in_=y_codes[h][:])
+
+        for r in range(PACK):
+            if r % 2 == 0:
+                nc.scalar.copy(out=y[0][:, r, :], in_=acc[r][:, 0:HALF])
+            else:
+                nc.vector.tensor_copy(out=y[0][:, r, :], in_=acc[r][:, 0:HALF])
+        nc.sync.dma_start(out=out_rows[:, :, 0:HALF], in_=y[0][:])
+        for r in range(PACK):
+            nc.scalar.copy(out=y[1][:, r, :], in_=acc[r][:, HALF:T])
+        finish(0)
+        nc.scalar.dma_start(out=out_rows[:, :, HALF:T], in_=y[1][:])
+        finish(1)
+        ys_words = y_scales[:].bitcast(I32)
+        out_scales = out_2[0].bitcast(I32)
+        for q in range(4):
+            engine = nc.sync if q % 2 == 0 else nc.scalar
+            engine.dma_start(out=out_scales[4 * q : 4 * q + 4, :], in_=ys_words[32 * q : 32 * q + 4, :])

@@ -19,7 +19,9 @@ P = 128
 PACK = 4
 PASSES = K // (P * PACK)
 HALF = T // 2
+QUARTER = T // 4
 WA_ROW = 4
+LAST_SPLIT = 416
 
 
 def tile_mix_kept_and_cut_off_pl_kernel(tc, xf, lo, hi, fa, fb, wa_words, wa_scales, wb_words, wb_scales, out_0, out_1, out_2):
@@ -32,14 +34,19 @@ def tile_mix_kept_and_cut_off_pl_kernel(tc, xf, lo, hi, fa, fb, wa_words, wa_sca
         def tile(name, shape, dtype):
             return sb.tile(shape, dtype, name=name, align_bytes=64)
 
-        slots = [(z, j) for z in range(PASSES) for j in range(PACK)]
-        x = {s: tile("x%d%d" % s, [P, T], F32) for s in slots}
-        b = {s: tile("b%d%d" % s, [P, T], F32) for s in slots}
-        d = {s: tile("d%d%d" % s, [P, T], F32) for s in slots}
+        x = [tile("x%d" % z, [P, PACK, T], F32) for z in range(PASSES)]
+        b = [tile("b%d" % z, [P, PACK, T], F32) for z in range(PASSES)]
+        d = [tile("d%d" % z, [P, PACK, T], F32) for z in range(PASSES)]
         par = {n: tile(n, [P, PASSES, PACK], F32) for n in ("hi", "lo", "fa", "fb")}
         ops = [(o, z) for o in ("a", "c") for z in range(PASSES)]
-        rows = {s: tile("rows%s%d" % s, [P, PACK, T], BF16) for s in ops}
-        grouped = {(o, z, h): tile("grp%s%d%d" % (o, z, h), [P, HALF * PACK], BF16) for o, z in ops for h in range(2)}
+        parts = {("c", 0): [(0, T)], ("a", 0): [(0, T)], ("c", 1): [(0, HALF), (HALF, T)], ("a", 1): [(0, HALF), (HALF, T)]}
+        row_parts = {("c", 0): [(0, T)], ("a", 0): [(0, T)], ("c", 1): [(0, T)], ("a", 1): [(0, HALF), (HALF, T)]}
+        rows = {(o, z, t0): tile("rows%s%d_%d" % (o, z, t0), [P, PACK, t1 - t0], BF16) for o, z in ops for t0, t1 in row_parts[o, z]}
+        grouped = {(o, z, t0): tile("grp%s%d_%d" % (o, z, t0), [P, (t1 - t0) * PACK], BF16) for o, z in ops for t0, t1 in parts[o, z]}
+
+        def first(table, o, z, t):
+            return max(t0 for t0, t1 in table[o, z] if t0 <= t)
+
         codes = {s: tile("codes%s%d" % s, [P, T], I32) for s in ops}
         scales = {s: tile("scales%s%d" % s, [P, T], U8) for s in ops}
         wa_raw = tile("wa_raw", [P, PASSES * N], I32)
@@ -48,20 +55,38 @@ def tile_mix_kept_and_cut_off_pl_kernel(tc, xf, lo, hi, fa, fb, wa_words, wa_sca
         wa = tile("wa", [P, PASSES * N], I32)
         wb = tile("wb", [P, PASSES * 2 * N], U8)
         ws = tile("ws", [P, PASSES * N], U8)
+        warm_in = tile("warm_in", [P, 1], F32)
+        warm_out = tile("warm_out", [P, 1], F32)
         acc = [psum.tile([P, T], F32, name="acc%d" % r) for r in range(PACK)]
         y = [tile("y%d" % h, [P, PACK, HALF], F32) for h in range(2)]
         y_grouped = [tile("yg%d" % h, [P, HALF * PACK], BF16) for h in range(2)]
         y_codes = [tile("yc%d" % h, [P, HALF], I32) for h in range(2)]
         y_scales = tile("ys", [P, T], U8)
 
+        nc.vector.memset(warm_in[:], 0.0)
         nc.vector.memset(ws_raw[:].bitcast(I32), 0)
 
-        for name, src in (("hi", hi), ("lo", lo), ("fa", fa), ("fb", fb)):
-            nc.scalar.dma_start(out=par[name][:], in_=src.rearrange("(z p j) o -> p z (j o)", p=P, j=PACK))
-        x_rows = xf.rearrange("(z p j) t -> z j p t", p=P, j=PACK)
-        for z, j in slots:
-            nc.sync.dma_start(out=x[z, j][:], in_=x_rows[z, j])
-        nc.sync.dma_start(out=wa_raw[:].rearrange("p (z c) -> p z c", z=PASSES), in_=wa_words.rearrange("z p c r -> p z (c r)").bitcast(I32))
+        def load_par(engine, name, src):
+            engine.dma_start(out=par[name][:], in_=src.rearrange("(z p j) o -> p z (j o)", p=P, j=PACK))
+
+        x_rows = xf.rearrange("(z p j) t -> z p j t", p=P, j=PACK)
+
+        def load_x(z, j0, j1, t0=0, t1=T):
+            nc.sync.dma_start(out=x[z][:, j0:j1, t0:t1], in_=x_rows[z, :, j0:j1, t0:t1])
+
+        load_par(nc.scalar, "hi", hi)
+        load_x(0, 0, 1, 0, HALF)
+        load_par(nc.scalar, "lo", lo)
+        load_x(0, 0, 1, HALF, T)
+        load_par(nc.scalar, "fa", fa)
+        load_x(0, 1, 2)
+        load_par(nc.scalar, "fb", fb)
+        nc.scalar.activation(out=warm_out[:], in_=warm_in[:], func=COPY)
+        load_x(0, 2, 3)
+        load_x(0, 3, 4)
+        load_x(1, 0, 2)
+        load_x(1, 2, 4)
+        nc.sync.dma_start(out=wb_raw[:].bitcast(I32).rearrange("p (z c) -> p z c", z=PASSES), in_=wb_words.rearrange("z p c -> p z c").bitcast(I32))
         ws_words = ws_raw[:].bitcast(I32).rearrange("p (z c) -> p z c", z=PASSES)
         for row0, src in ((WA_ROW, wa_scales), (0, wb_scales)):
             for q in range(4):
@@ -69,21 +94,20 @@ def tile_mix_kept_and_cut_off_pl_kernel(tc, xf, lo, hi, fa, fb, wa_words, wa_sca
                     out=ws_words[32 * q + row0 : 32 * q + row0 + 4],
                     in_=src[:, 4 * q : 4 * q + 4, :].rearrange("z r c -> r z c").bitcast(I32),
                 )
-        nc.sync.dma_start(out=wb_raw[:].bitcast(I32).rearrange("p (z c) -> p z c", z=PASSES), in_=wb_words.rearrange("z p c -> p z c").bitcast(I32))
+        nc.sync.dma_start(out=wa_raw[:].rearrange("p (z c) -> p z c", z=PASSES), in_=wa_words.rearrange("z p c r -> p z (c r)").bitcast(I32))
 
         def col(name, z, j):
             return par[name][:, z, j : j + 1]
 
-        def clamp(z, j):
-            nc.vector.tensor_scalar(out=b[z, j][:], in0=x[z, j][:], scalar1=col("hi", z, j), scalar2=col("lo", z, j), op0=ALU.min, op1=ALU.max)
+        def clamp(z, j, t0=0, t1=T):
+            nc.vector.tensor_scalar(out=b[z][:, j, t0:t1], in0=x[z][:, j, t0:t1], scalar1=col("hi", z, j), scalar2=col("lo", z, j), op0=ALU.min, op1=ALU.max)
 
-        def cut(z, j):
-            nc.vector.tensor_tensor(out=d[z, j][:], in0=x[z, j][:], in1=b[z, j][:], op=ALU.subtract)
+        def cut(z, j0, j1, t0=0, t1=T):
+            nc.vector.tensor_tensor(out=d[z][:, j0:j1, t0:t1], in0=x[z][:, j0:j1, t0:t1], in1=b[z][:, j0:j1, t0:t1], op=ALU.subtract)
 
-        def scale_rows(o, z):
+        def scale_row(o, z, j, t0=0, t1=T):
             src, factor = (b, "fa") if o == "a" else (d, "fb")
-            for j in range(PACK):
-                nc.scalar.activation(out=rows[o, z][:, j, :], in_=src[z, j][:], func=COPY, scale=col(factor, z, j))
+            nc.scalar.activation(out=rows[o, z, t0][:, j, :], in_=src[z][:, j, t0:t1], func=COPY, scale=col(factor, z, j))
 
         def interleave(engine, dst, src):
             out = dst.rearrange("p (c i j) -> p c j i", i=4, j=PACK)
@@ -93,12 +117,12 @@ def tile_mix_kept_and_cut_off_pl_kernel(tc, xf, lo, hi, fa, fb, wa_words, wa_sca
             else:
                 nc.scalar.copy(out=out, in_=in_)
 
-        def group(engine, o, z, h):
-            interleave(engine, grouped[o, z, h][:], rows[o, z][:, :, h * HALF : (h + 1) * HALF])
+        def group(engine, o, z, t0=0, t1=T):
+            g0, r0 = first(parts, o, z, t0), first(row_parts, o, z, t0)
+            interleave(engine, grouped[o, z, g0][:, PACK * (t0 - g0) : PACK * (t1 - g0)], rows[o, z, r0][:, :, t0 - r0 : t1 - r0])
 
-        def quantize(o, z, h):
-            cols = slice(h * HALF, (h + 1) * HALF)
-            nc.vector.quantize_mx(out=codes[o, z][:, cols].bitcast(E4M3 if o == "a" else E5M2), scales=scales[o, z][:, cols], in_=grouped[o, z, h][:])
+        def quantize(o, z, t0=0, t1=T):
+            nc.vector.quantize_mx(out=codes[o, z][:, t0:t1].bitcast(E4M3 if o == "a" else E5M2), scales=scales[o, z][:, t0:t1], in_=grouped[o, z, t0][:])
 
         def deal_wa():
             nc.vector.tensor_copy(out=wa[:].rearrange("p (r c i) -> p c r i", r=PACK, i=4), in_=wa_raw[:].rearrange("p (c i r) -> p c r i", r=PACK, i=4))
@@ -109,72 +133,99 @@ def tile_mix_kept_and_cut_off_pl_kernel(tc, xf, lo, hi, fa, fb, wa_words, wa_sca
         def deal_scales():
             nc.vector.tensor_copy(out=ws[:].rearrange("p (r m) -> p r m", r=PACK), in_=ws_raw[:].rearrange("p (m r) -> p r m", r=PACK))
 
-        def multiply(o, z, start=False, stop=False):
+        def multiply(o, z, t0=0, t1=T, start=False, stop=False):
             for r in range(PACK):
                 c0 = (r * PASSES + z) * P
                 if o == "a":
                     lhs, lhs_scale, fmt = wa[:, c0 : c0 + P].bitcast(E4M3), ws[WA_ROW:P, c0 : c0 + P], E4M3
                 else:
                     lhs, lhs_scale, fmt = wb[:, 2 * c0 : 2 * c0 + 2 * P].bitcast(E2M1), ws[:, c0 : c0 + P], E5M2
-                nc.tensor.matmul_mx(out=acc[r][:], lhsT=lhs, lhsT_scale=lhs_scale, rhs=codes[o, z][:].bitcast(fmt), rhs_scale=scales[o, z][:], start=start, stop=stop)
+                nc.tensor.matmul_mx(out=acc[r][:, t0:t1], lhsT=lhs, lhsT_scale=lhs_scale, rhs=codes[o, z][:, t0:t1].bitcast(fmt), rhs_scale=scales[o, z][:, t0:t1], start=start, stop=stop)
 
-        clamp(*slots[0])
-        for prev, cur in zip(slots[:-2], slots[1:-1]):
-            clamp(*cur)
-            cut(*prev)
-        clamp(*slots[-1])
-        cut(*slots[-2])
-        scale_rows("a", 0)
-        scale_rows("c", 0)
-        group("scalar", "a", 0, 0)
-        group("scalar", "a", 0, 1)
-        deal_wa()
-        cut(*slots[-1])
-        scale_rows("c", 1)
-        scale_rows("a", 1)
-        group("scalar", "a", 1, 1)
-        deal_scales()
-        quantize("a", 0, 0)
-        quantize("a", 0, 1)
-        multiply("a", 0, start=True)
-        group("vector", "c", 0, 0)
-        group("vector", "c", 0, 1)
+        clamp(0, 0, 0, HALF)
+        clamp(0, 0, HALF, T)
+        cut(0, 0, 1, 0, HALF)
+        cut(0, 0, 1, HALF, T)
+        clamp(0, 1)
+        clamp(0, 2)
+        cut(0, 1, 2)
+        clamp(0, 3)
+        cut(0, 2, 3)
+        clamp(1, 0)
+        cut(0, 3, 4)
+        for o, j in (("a", 0), ("c", 0), ("a", 1), ("a", 2), ("c", 1), ("a", 3), ("c", 2), ("c", 3)):
+            scale_row(o, 0, j)
+        group("scalar", "c", 0)
+        clamp(1, 1)
+        clamp(1, 2)
+        clamp(1, 3)
+        cut(1, 0, 2)
+        cut(1, 2, 4)
         deal_wb()
-        quantize("c", 0, 0)
-        quantize("c", 0, 1)
-        multiply("c", 0)
-        group("vector", "c", 1, 0)
-        group("vector", "c", 1, 1)
-        quantize("c", 1, 0)
-        quantize("c", 1, 1)
+        deal_scales()
+        for j in range(PACK):
+            scale_row("c", 1, j)
+        group("scalar", "a", 0, QUARTER, T)
+        for t0 in (0, HALF):
+            for j in range(PACK):
+                scale_row("a", 1, j, t0, t0 + HALF)
+        quantize("c", 0)
+        multiply("c", 0, start=True)
+        group("vector", "c", 1, 0, HALF)
+        group("vector", "c", 1, HALF, T)
+        quantize("c", 1, 0, HALF)
+        quantize("c", 1, HALF, T)
         multiply("c", 1)
-        group("vector", "a", 1, 0)
-        quantize("a", 1, 1)
-        quantize("a", 1, 0)
-        multiply("a", 1, stop=True)
+        group("vector", "a", 0, 0, QUARTER)
+        deal_wa()
+        quantize("a", 0)
+        multiply("a", 0)
+        group("vector", "a", 1, 0, HALF)
+        quantize("a", 1, 0, HALF)
+        multiply("a", 1, 0, HALF)
+        group("scalar", "a", 1, LAST_SPLIT, T)
+        group("vector", "a", 1, HALF, LAST_SPLIT)
+        quantize("a", 1, HALF, T)
+        multiply("a", 1, HALF, T, stop=True)
 
         out_rows = out_0.rearrange("(p r) t -> p r t", r=PACK)
         out_words = out_1.rearrange("z p c r -> p (z c r)").bitcast(I32)
 
-        def finish(h):
+        def drain(engine, r, h):
             cols = slice(h * HALF, (h + 1) * HALF)
-            interleave("vector", y_grouped[h][:], y[h][:])
-            nc.vector.quantize_mx(out=y_codes[h][:].bitcast(E4M3), scales=y_scales[:, cols], in_=y_grouped[h][:])
-            nc.sync.dma_start(out=out_words[:, cols], in_=y_codes[h][:])
-
-        for r in range(PACK):
-            if r % 2 == 0:
-                nc.scalar.copy(out=y[0][:, r, :], in_=acc[r][:, 0:HALF])
+            if engine == "vector":
+                nc.vector.tensor_copy(out=y[h][:, r, :], in_=acc[r][:, cols])
             else:
-                nc.vector.tensor_copy(out=y[0][:, r, :], in_=acc[r][:, 0:HALF])
-        nc.sync.dma_start(out=out_rows[:, :, 0:HALF], in_=y[0][:])
-        for r in range(PACK):
-            nc.scalar.copy(out=y[1][:, r, :], in_=acc[r][:, HALF:T])
-        finish(0)
-        nc.scalar.dma_start(out=out_rows[:, :, HALF:T], in_=y[1][:])
-        finish(1)
+                nc.scalar.copy(out=y[h][:, r, :], in_=acc[r][:, cols])
+
+        def store(h, r0, r1):
+            nc.sync.dma_start(out=out_rows[:, r0:r1, h * HALF : (h + 1) * HALF], in_=y[h][:, r0:r1, :])
+
+        def group_result(engine, h, t0, t1):
+            interleave(engine, y_grouped[h][:, PACK * t0 : PACK * t1], y[h][:, :, t0:t1])
+
+        def quantize_result(h):
+            cols = slice(h * HALF, (h + 1) * HALF)
+            nc.vector.quantize_mx(out=y_codes[h][:].bitcast(E4M3), scales=y_scales[:, cols], in_=y_grouped[h][:])
+            nc.scalar.dma_start(out=out_words[:, cols], in_=y_codes[h][:])
+
+        drain("scalar", 0, 0)
+        drain("vector", 1, 0)
+        store(0, 0, 2)
+        drain("scalar", 2, 0)
+        drain("vector", 3, 0)
+        store(0, 2, 4)
+        drain("vector", 3, 1)
+        for r in range(3):
+            drain("scalar", r, 1)
+        store(1, 0, 4)
+        group_result("vector", 0, 0, HALF)
+        group_result("vector", 1, 0, QUARTER)
+        group_result("scalar", 1, QUARTER, HALF)
+        quantize_result(0)
+        quantize_result(1)
         ys_words = y_scales[:].bitcast(I32)
         out_scales = out_2[0].bitcast(I32)
         for q in range(4):
-            engine = nc.sync if q % 2 == 0 else nc.scalar
+            engine = nc.scalar if q == 3 else nc.sync
             engine.dma_start(out=out_scales[4 * q : 4 * q + 4, :], in_=ys_words[32 * q : 32 * q + 4, :])

@@ -21,7 +21,7 @@ PASSES = K // (P * PACK)
 HALF = T // 2
 QUARTER = T // 4
 WA_ROW = 4
-LAST_SPLIT = 416
+LAST_SPLIT = 160
 
 
 def tile_mix_kept_and_cut_off_pl_kernel(tc, xf, lo, hi, fa, fb, wa_words, wa_scales, wb_words, wb_scales, out_0, out_1, out_2):
@@ -34,13 +34,19 @@ def tile_mix_kept_and_cut_off_pl_kernel(tc, xf, lo, hi, fa, fb, wa_words, wa_sca
         def tile(name, shape, dtype):
             return sb.tile(shape, dtype, name=name, align_bytes=64)
 
-        x = [tile("x%d" % z, [P, PACK, T], F32) for z in range(PASSES)]
-        b = [tile("b%d" % z, [P, PACK, T], F32) for z in range(PASSES)]
-        d = [tile("d%d" % z, [P, PACK, T], F32) for z in range(PASSES)]
+        spans = [(0, 0, T), (1, 0, HALF), (1, HALF, T)]
+        x = {(z, t0): tile("x%d_%d" % (z, t0), [P, PACK, t1 - t0], F32) for z, t0, t1 in spans}
+        b = {(z, t0): tile("b%d_%d" % (z, t0), [P, PACK, t1 - t0], F32) for z, t0, t1 in spans}
+        d = {(z, t0): tile("d%d_%d" % (z, t0), [P, PACK, t1 - t0], F32) for z, t0, t1 in spans}
+
+        def view(tiles, z, j0, j1, t0, t1):
+            base = 0 if z == 0 else t0 // HALF * HALF
+            return tiles[z, base][:, j0:j1, t0 - base : t1 - base]
+
         par = {n: tile(n, [P, PASSES, PACK], F32) for n in ("hi", "lo", "fa", "fb")}
         ops = [(o, z) for o in ("a", "c") for z in range(PASSES)]
         parts = {("c", 0): [(0, T)], ("a", 0): [(0, T)], ("c", 1): [(0, HALF), (HALF, T)], ("a", 1): [(0, HALF), (HALF, T)]}
-        row_parts = {("c", 0): [(0, T)], ("a", 0): [(0, T)], ("c", 1): [(0, T)], ("a", 1): [(0, HALF), (HALF, T)]}
+        row_parts = {("c", 0): [(0, T)], ("a", 0): [(0, T)], ("c", 1): [(0, HALF), (HALF, T)], ("a", 1): [(0, HALF), (HALF, T)]}
         rows = {(o, z, t0): tile("rows%s%d_%d" % (o, z, t0), [P, PACK, t1 - t0], BF16) for o, z in ops for t0, t1 in row_parts[o, z]}
         grouped = {(o, z, t0): tile("grp%s%d_%d" % (o, z, t0), [P, (t1 - t0) * PACK], BF16) for o, z in ops for t0, t1 in parts[o, z]}
 
@@ -57,7 +63,7 @@ def tile_mix_kept_and_cut_off_pl_kernel(tc, xf, lo, hi, fa, fb, wa_words, wa_sca
         ws = tile("ws", [P, PASSES * N], U8)
         warm_in = tile("warm_in", [P, 1], F32)
         warm_out = tile("warm_out", [P, 1], F32)
-        acc = [psum.tile([P, T], F32, name="acc%d" % r) for r in range(PACK)]
+        acc = {(h, r): psum.tile([P, T], F32, name="acc%d%d" % (h, r)) for h in range(2) for r in range(PACK)}
         y = [tile("y%d" % h, [P, PACK, HALF], F32) for h in range(2)]
         y_grouped = [tile("yg%d" % h, [P, HALF * PACK], BF16) for h in range(2)]
         y_codes = [tile("yc%d" % h, [P, HALF], I32) for h in range(2)]
@@ -65,6 +71,8 @@ def tile_mix_kept_and_cut_off_pl_kernel(tc, xf, lo, hi, fa, fb, wa_words, wa_sca
 
         nc.vector.memset(warm_in[:], 0.0)
         nc.vector.memset(ws_raw[:].bitcast(I32), 0)
+        nc.vector.memset(codes["c", 1][:, HALF:T], 0)
+        nc.vector.memset(scales["c", 1][:, HALF:T].bitcast(I32), 0)
 
         def load_par(engine, name, src):
             engine.dma_start(out=par[name][:], in_=src.rearrange("(z p j) o -> p z (j o)", p=P, j=PACK))
@@ -72,7 +80,7 @@ def tile_mix_kept_and_cut_off_pl_kernel(tc, xf, lo, hi, fa, fb, wa_words, wa_sca
         x_rows = xf.rearrange("(z p j) t -> z p j t", p=P, j=PACK)
 
         def load_x(z, j0, j1, t0=0, t1=T):
-            nc.sync.dma_start(out=x[z][:, j0:j1, t0:t1], in_=x_rows[z, :, j0:j1, t0:t1])
+            nc.sync.dma_start(out=view(x, z, j0, j1, t0, t1), in_=x_rows[z, :, j0:j1, t0:t1])
 
         load_par(nc.scalar, "hi", hi)
         load_x(0, 0, 1, 0, HALF)
@@ -84,30 +92,38 @@ def tile_mix_kept_and_cut_off_pl_kernel(tc, xf, lo, hi, fa, fb, wa_words, wa_sca
         nc.scalar.activation(out=warm_out[:], in_=warm_in[:], func=COPY)
         load_x(0, 2, 3)
         load_x(0, 3, 4)
-        load_x(1, 0, 2)
-        load_x(1, 2, 4)
-        nc.sync.dma_start(out=wb_raw[:].bitcast(I32).rearrange("p (z c) -> p z c", z=PASSES), in_=wb_words.rearrange("z p c -> p z c").bitcast(I32))
         ws_words = ws_raw[:].bitcast(I32).rearrange("p (z c) -> p z c", z=PASSES)
-        for row0, src in ((WA_ROW, wa_scales), (0, wb_scales)):
+
+        def load_scales(engine, row0, src):
             for q in range(4):
-                nc.sync.dma_start(
+                engine.dma_start(
                     out=ws_words[32 * q + row0 : 32 * q + row0 + 4],
                     in_=src[:, 4 * q : 4 * q + 4, :].rearrange("z r c -> r z c").bitcast(I32),
                 )
+
+        load_scales(nc.gpsimd, 0, wb_scales)
+        load_x(1, 0, 4, 0, HALF)
+        nc.sync.dma_start(out=wb_raw[:].bitcast(I32).rearrange("p (z c) -> p z c", z=PASSES), in_=wb_words.bitcast(I32).rearrange("z p c -> p z c"))
+        load_scales(nc.sync, WA_ROW, wa_scales)
+        load_x(1, 0, 4, HALF, T)
         nc.sync.dma_start(out=wa_raw[:].rearrange("p (z c) -> p z c", z=PASSES), in_=wa_words.rearrange("z p c r -> p z (c r)").bitcast(I32))
 
         def col(name, z, j):
             return par[name][:, z, j : j + 1]
 
         def clamp(z, j, t0=0, t1=T):
-            nc.vector.tensor_scalar(out=b[z][:, j, t0:t1], in0=x[z][:, j, t0:t1], scalar1=col("hi", z, j), scalar2=col("lo", z, j), op0=ALU.min, op1=ALU.max)
+            nc.vector.tensor_scalar(out=view(b, z, j, j + 1, t0, t1), in0=view(x, z, j, j + 1, t0, t1), scalar1=col("hi", z, j), scalar2=col("lo", z, j), op0=ALU.min, op1=ALU.max)
 
         def cut(z, j0, j1, t0=0, t1=T):
-            nc.vector.tensor_tensor(out=d[z][:, j0:j1, t0:t1], in0=x[z][:, j0:j1, t0:t1], in1=b[z][:, j0:j1, t0:t1], op=ALU.subtract)
+            nc.vector.tensor_tensor(out=view(d, z, j0, j1, t0, t1), in0=view(x, z, j0, j1, t0, t1), in1=view(b, z, j0, j1, t0, t1), op=ALU.subtract)
 
-        def scale_row(o, z, j, t0=0, t1=T):
+        def scale_row(engine, o, z, j, t0=0, t1=T):
             src, factor = (b, "fa") if o == "a" else (d, "fb")
-            nc.scalar.activation(out=rows[o, z, t0][:, j, :], in_=src[z][:, j, t0:t1], func=COPY, scale=col(factor, z, j))
+            out, in_ = rows[o, z, t0][:, j : j + 1, :], view(src, z, j, j + 1, t0, t1)
+            if engine == "vector":
+                nc.vector.tensor_scalar(out=out, in0=in_, scalar1=col(factor, z, j), scalar2=None, op0=ALU.mult)
+            else:
+                nc.scalar.activation(out=out, in_=in_, func=COPY, scale=col(factor, z, j))
 
         def interleave(engine, dst, src):
             out = dst.rearrange("p (c i j) -> p c j i", i=4, j=PACK)
@@ -133,60 +149,15 @@ def tile_mix_kept_and_cut_off_pl_kernel(tc, xf, lo, hi, fa, fb, wa_words, wa_sca
         def deal_scales():
             nc.vector.tensor_copy(out=ws[:].rearrange("p (r m) -> p r m", r=PACK), in_=ws_raw[:].rearrange("p (m r) -> p r m", r=PACK))
 
-        def multiply(o, z, t0=0, t1=T, start=False, stop=False):
+        def multiply(o, z, h):
+            cols = slice(h * HALF, (h + 1) * HALF) if o == "a" else slice(0, T)
             for r in range(PACK):
                 c0 = (r * PASSES + z) * P
                 if o == "a":
                     lhs, lhs_scale, fmt = wa[:, c0 : c0 + P].bitcast(E4M3), ws[WA_ROW:P, c0 : c0 + P], E4M3
                 else:
                     lhs, lhs_scale, fmt = wb[:, 2 * c0 : 2 * c0 + 2 * P].bitcast(E2M1), ws[:, c0 : c0 + P], E5M2
-                nc.tensor.matmul_mx(out=acc[r][:, t0:t1], lhsT=lhs, lhsT_scale=lhs_scale, rhs=codes[o, z][:, t0:t1].bitcast(fmt), rhs_scale=scales[o, z][:, t0:t1], start=start, stop=stop)
-
-        clamp(0, 0, 0, HALF)
-        clamp(0, 0, HALF, T)
-        cut(0, 0, 1, 0, HALF)
-        cut(0, 0, 1, HALF, T)
-        clamp(0, 1)
-        clamp(0, 2)
-        cut(0, 1, 2)
-        clamp(0, 3)
-        cut(0, 2, 3)
-        clamp(1, 0)
-        cut(0, 3, 4)
-        for o, j in (("a", 0), ("c", 0), ("a", 1), ("a", 2), ("c", 1), ("a", 3), ("c", 2), ("c", 3)):
-            scale_row(o, 0, j)
-        group("scalar", "c", 0)
-        clamp(1, 1)
-        clamp(1, 2)
-        clamp(1, 3)
-        cut(1, 0, 2)
-        cut(1, 2, 4)
-        deal_wb()
-        deal_scales()
-        for j in range(PACK):
-            scale_row("c", 1, j)
-        group("scalar", "a", 0, QUARTER, T)
-        for t0 in (0, HALF):
-            for j in range(PACK):
-                scale_row("a", 1, j, t0, t0 + HALF)
-        quantize("c", 0)
-        multiply("c", 0, start=True)
-        group("vector", "c", 1, 0, HALF)
-        group("vector", "c", 1, HALF, T)
-        quantize("c", 1, 0, HALF)
-        quantize("c", 1, HALF, T)
-        multiply("c", 1)
-        group("vector", "a", 0, 0, QUARTER)
-        deal_wa()
-        quantize("a", 0)
-        multiply("a", 0)
-        group("vector", "a", 1, 0, HALF)
-        quantize("a", 1, 0, HALF)
-        multiply("a", 1, 0, HALF)
-        group("scalar", "a", 1, LAST_SPLIT, T)
-        group("vector", "a", 1, HALF, LAST_SPLIT)
-        quantize("a", 1, HALF, T)
-        multiply("a", 1, HALF, T, stop=True)
+                nc.tensor.matmul_mx(out=acc[h, r][:, cols], lhsT=lhs, lhsT_scale=lhs_scale, rhs=codes[o, z][:, cols].bitcast(fmt), rhs_scale=scales[o, z][:, cols], start=(o, z) == ("c", 0), stop=(o, z) == ("a", 1))
 
         out_rows = out_0.rearrange("(p r) t -> p r t", r=PACK)
         out_words = out_1.rearrange("z p c r -> p (z c r)").bitcast(I32)
@@ -194,9 +165,9 @@ def tile_mix_kept_and_cut_off_pl_kernel(tc, xf, lo, hi, fa, fb, wa_words, wa_sca
         def drain(engine, r, h):
             cols = slice(h * HALF, (h + 1) * HALF)
             if engine == "vector":
-                nc.vector.tensor_copy(out=y[h][:, r, :], in_=acc[r][:, cols])
+                nc.vector.tensor_copy(out=y[h][:, r, :], in_=acc[h, r][:, cols])
             else:
-                nc.scalar.copy(out=y[h][:, r, :], in_=acc[r][:, cols])
+                nc.scalar.copy(out=y[h][:, r, :], in_=acc[h, r][:, cols])
 
         def store(h, r0, r1):
             nc.sync.dma_start(out=out_rows[:, r0:r1, h * HALF : (h + 1) * HALF], in_=y[h][:, r0:r1, :])
@@ -204,26 +175,79 @@ def tile_mix_kept_and_cut_off_pl_kernel(tc, xf, lo, hi, fa, fb, wa_words, wa_sca
         def group_result(engine, h, t0, t1):
             interleave(engine, y_grouped[h][:, PACK * t0 : PACK * t1], y[h][:, :, t0:t1])
 
-        def quantize_result(h):
+        def quantize_result(h, engine):
             cols = slice(h * HALF, (h + 1) * HALF)
             nc.vector.quantize_mx(out=y_codes[h][:].bitcast(E4M3), scales=y_scales[:, cols], in_=y_grouped[h][:])
-            nc.scalar.dma_start(out=out_words[:, cols], in_=y_codes[h][:])
+            engine.dma_start(out=out_words[:, cols], in_=y_codes[h][:])
 
-        drain("scalar", 0, 0)
-        drain("vector", 1, 0)
+        A, B = (0, HALF), (HALF, T)
+        clamp(0, 0, *A)
+        clamp(0, 0, *B)
+        cut(0, 0, 1, *A)
+        cut(0, 0, 1, *B)
+        clamp(0, 1)
+        clamp(0, 2)
+        cut(0, 1, 2)
+        clamp(0, 3)
+        cut(0, 2, 3)
+        cut(0, 3, 4)
+        for o, j in (("a", 0), ("c", 0), ("a", 1), ("a", 2), ("c", 1), ("c", 2), ("c", 3)):
+            scale_row("scalar", o, 0, j)
+        for j in range(PACK):
+            clamp(1, j, *A)
+        deal_wb()
+        scale_row("scalar", "a", 0, 3)
+        group("scalar", "c", 0, *B)
+        group("vector", "c", 0, *A)
+        deal_scales()
+        quantize("c", 0)
+        multiply("c", 0, 0)
+        multiply("c", 0, 1)
+        cut(1, 0, 4, *A)
+        group("scalar", "a", 0)
+        deal_wa()
+        for j in range(PACK):
+            scale_row("vector", "c", 1, j, *A)
+        for j in range(PACK):
+            scale_row("scalar", "a", 1, j, *A)
+        group("scalar", "c", 1, *A)
+        for j in range(PACK):
+            clamp(1, j, *B)
+        quantize("a", 0)
+        multiply("a", 0, 0)
+        multiply("a", 0, 1)
+        group("scalar", "a", 1, *A)
+        cut(1, 0, 4, *B)
+        quantize("c", 1, *A)
+        multiply("c", 1, 0)
+        for j in range(PACK):
+            scale_row("vector", "c", 1, j, *B)
+        for j in range(PACK):
+            scale_row("scalar", "a", 1, j, *B)
+        quantize("a", 1, *A)
+        multiply("a", 1, 0)
+        group("vector", "c", 1, *B)
+        drain("vector", 0, 0)
+        quantize("c", 1, *B)
+        multiply("c", 1, 1)
+        group("vector", "a", 1, *B)
+        drain("scalar", 1, 0)
         store(0, 0, 2)
         drain("scalar", 2, 0)
-        drain("vector", 3, 0)
+        drain("scalar", 3, 0)
         store(0, 2, 4)
-        drain("vector", 3, 1)
-        for r in range(3):
-            drain("scalar", r, 1)
-        store(1, 0, 4)
-        group_result("vector", 0, 0, HALF)
-        group_result("vector", 1, 0, QUARTER)
-        group_result("scalar", 1, QUARTER, HALF)
-        quantize_result(0)
-        quantize_result(1)
+        group_result("vector", 0, 0, LAST_SPLIT)
+        group_result("scalar", 0, LAST_SPLIT, HALF)
+        quantize("a", 1, *B)
+        multiply("a", 1, 1)
+        quantize_result(0, nc.sync)
+        for r in range(PACK):
+            drain("vector" if r % 2 == 0 else "scalar", r, 1)
+            if r % 2 == 1:
+                store(1, r - 1, r + 1)
+        group_result("vector", 1, 0, LAST_SPLIT)
+        group_result("scalar", 1, LAST_SPLIT, HALF)
+        quantize_result(1, nc.scalar)
         ys_words = y_scales[:].bitcast(I32)
         out_scales = out_2[0].bitcast(I32)
         for q in range(4):

from contextlib import ExitStack

import concourse.mybir as mybir

K, T, N = 1024, 512, 512
FLOPS = 2 * 2 * K * T * N

F32 = mybir.dt.float32
BF16 = mybir.dt.bfloat16
I32 = mybir.dt.int32
U8 = mybir.dt.uint8
E4M3 = mybir.dt.float8_e4m3fn_x4
E5M2 = mybir.dt.float8_e5m2_x4
E2M1 = mybir.dt.float4_e2m1fn_x4
ALU = mybir.AluOpType
COPY = mybir.ActivationFunctionType.Copy

P = 128
PACK = 4
PASSES = K // (P * PACK)
HALF = T // 2
QUARTER = T // 4
WA_ROW = 4
LAST_SPLIT = 160


def tile_mix_kept_and_cut_off_pl_kernel(tc, xf, lo, hi, fa, fb, wa_words, wa_scales, wb_words, wb_scales, out_0, out_1, out_2):
    nc = tc.nc
    with ExitStack() as ctx:
        sb = ctx.enter_context(tc.tile_pool(name="sb", bufs=1))
        psum = ctx.enter_context(tc.psum_pool(name="psum", bufs=1))
        ctx.enter_context(tc.manual_schedule())

        def tile(name, shape, dtype):
            return sb.tile(shape, dtype, name=name, align_bytes=64)

        spans = [(0, 0, T), (1, 0, HALF), (1, HALF, T)]
        x = {(z, t0): tile("x%d_%d" % (z, t0), [P, PACK, t1 - t0], F32) for z, t0, t1 in spans}
        b = {(z, t0): tile("b%d_%d" % (z, t0), [P, PACK, t1 - t0], F32) for z, t0, t1 in spans}
        d = {(z, t0): tile("d%d_%d" % (z, t0), [P, PACK, t1 - t0], F32) for z, t0, t1 in spans}

        def view(tiles, z, j0, j1, t0, t1):
            base = 0 if z == 0 else t0 // HALF * HALF
            return tiles[z, base][:, j0:j1, t0 - base : t1 - base]

        par = {n: tile(n, [P, PASSES, PACK], F32) for n in ("hi", "lo", "fa", "fb")}
        ops = [(o, z) for o in ("a", "c") for z in range(PASSES)]
        parts = {("c", 0): [(0, T)], ("a", 0): [(0, T)], ("c", 1): [(0, HALF), (HALF, T)], ("a", 1): [(0, HALF), (HALF, T)]}
        row_parts = {("c", 0): [(0, T)], ("a", 0): [(0, T)], ("c", 1): [(0, HALF), (HALF, T)], ("a", 1): [(0, HALF), (HALF, T)]}
        rows = {(o, z, t0): tile("rows%s%d_%d" % (o, z, t0), [P, PACK, t1 - t0], BF16) for o, z in ops for t0, t1 in row_parts[o, z]}
        grouped = {(o, z, t0): tile("grp%s%d_%d" % (o, z, t0), [P, (t1 - t0) * PACK], BF16) for o, z in ops for t0, t1 in parts[o, z]}

        def first(table, o, z, t):
            return max(t0 for t0, t1 in table[o, z] if t0 <= t)

        codes = {s: tile("codes%s%d" % s, [P, T], I32) for s in ops}
        scales = {s: tile("scales%s%d" % s, [P, T], U8) for s in ops}
        wa_raw = tile("wa_raw", [P, PASSES * N], I32)
        wb_raw = tile("wb_raw", [P, PASSES * 2 * N], U8)
        ws_raw = tile("ws_raw", [P, PASSES * N], U8)
        wa = tile("wa", [P, PASSES * N], I32)
        wb = tile("wb", [P, PASSES * 2 * N], U8)
        ws = tile("ws", [P, PASSES * N], U8)
        warm_in = tile("warm_in", [P, 1], F32)
        warm_out = tile("warm_out", [P, 1], F32)
        acc = {(h, r): psum.tile([P, T], F32, name="acc%d%d" % (h, r)) for h in range(2) for r in range(PACK)}
        y = [tile("y%d" % h, [P, PACK, HALF], F32) for h in range(2)]
        y_grouped = [tile("yg%d" % h, [P, HALF * PACK], BF16) for h in range(2)]
        y_codes = [tile("yc%d" % h, [P, HALF], I32) for h in range(2)]
        y_scales = tile("ys", [P, T], U8)

        nc.vector.memset(warm_in[:], 0.0)
        nc.vector.memset(ws_raw[:].bitcast(I32), 0)
        nc.vector.memset(codes["c", 1][:, HALF:T], 0)
        nc.vector.memset(scales["c", 1][:, HALF:T].bitcast(I32), 0)

        def load_par(engine, name, src):
            engine.dma_start(out=par[name][:], in_=src.rearrange("(z p j) o -> p z (j o)", p=P, j=PACK))

        x_rows = xf.rearrange("(z p j) t -> z p j t", p=P, j=PACK)

        def load_x(z, j0, j1, t0=0, t1=T):
            nc.sync.dma_start(out=view(x, z, j0, j1, t0, t1), in_=x_rows[z, :, j0:j1, t0:t1])

        load_par(nc.scalar, "hi", hi)
        load_x(0, 0, 1, 0, HALF)
        load_par(nc.scalar, "lo", lo)
        load_x(0, 0, 1, HALF, T)
        load_par(nc.scalar, "fa", fa)
        load_x(0, 1, 2)
        load_par(nc.scalar, "fb", fb)
        nc.scalar.activation(out=warm_out[:], in_=warm_in[:], func=COPY)
        load_x(0, 2, 3)
        load_x(0, 3, 4)
        ws_words = ws_raw[:].bitcast(I32).rearrange("p (z c) -> p z c", z=PASSES)

        def load_scales(engine, row0, src):
            for q in range(4):
                engine.dma_start(
                    out=ws_words[32 * q + row0 : 32 * q + row0 + 4],
                    in_=src[:, 4 * q : 4 * q + 4, :].rearrange("z r c -> r z c").bitcast(I32),
                )

        load_scales(nc.gpsimd, 0, wb_scales)
        load_x(1, 0, 4, 0, HALF)
        nc.sync.dma_start(out=wb_raw[:].bitcast(I32).rearrange("p (z c) -> p z c", z=PASSES), in_=wb_words.bitcast(I32).rearrange("z p c -> p z c"))
        load_scales(nc.sync, WA_ROW, wa_scales)
        load_x(1, 0, 4, HALF, T)
        nc.sync.dma_start(out=wa_raw[:].rearrange("p (z c) -> p z c", z=PASSES), in_=wa_words.rearrange("z p c r -> p z (c r)").bitcast(I32))

        def col(name, z, j):
            return par[name][:, z, j : j + 1]

        def clamp(z, j, t0=0, t1=T):
            nc.vector.tensor_scalar(out=view(b, z, j, j + 1, t0, t1), in0=view(x, z, j, j + 1, t0, t1), scalar1=col("hi", z, j), scalar2=col("lo", z, j), op0=ALU.min, op1=ALU.max)

        def cut(z, j0, j1, t0=0, t1=T):
            nc.vector.tensor_tensor(out=view(d, z, j0, j1, t0, t1), in0=view(x, z, j0, j1, t0, t1), in1=view(b, z, j0, j1, t0, t1), op=ALU.subtract)

        def scale_row(engine, o, z, j, t0=0, t1=T):
            src, factor = (b, "fa") if o == "a" else (d, "fb")
            out, in_ = rows[o, z, t0][:, j : j + 1, :], view(src, z, j, j + 1, t0, t1)
            if engine == "vector":
                nc.vector.tensor_scalar(out=out, in0=in_, scalar1=col(factor, z, j), scalar2=None, op0=ALU.mult)
            else:
                nc.scalar.activation(out=out, in_=in_, func=COPY, scale=col(factor, z, j))

        def interleave(engine, dst, src):
            out = dst.rearrange("p (c i j) -> p c j i", i=4, j=PACK)
            in_ = src.rearrange("p j (c i) -> p c j i", i=4)
            if engine == "vector":
                nc.vector.tensor_copy(out=out, in_=in_)
            else:
                nc.scalar.copy(out=out, in_=in_)

        def group(engine, o, z, t0=0, t1=T):
            g0, r0 = first(parts, o, z, t0), first(row_parts, o, z, t0)
            interleave(engine, grouped[o, z, g0][:, PACK * (t0 - g0) : PACK * (t1 - g0)], rows[o, z, r0][:, :, t0 - r0 : t1 - r0])

        def quantize(o, z, t0=0, t1=T):
            nc.vector.quantize_mx(out=codes[o, z][:, t0:t1].bitcast(E4M3 if o == "a" else E5M2), scales=scales[o, z][:, t0:t1], in_=grouped[o, z, t0][:])

        def deal_wa():
            nc.vector.tensor_copy(out=wa[:].rearrange("p (r c i) -> p c r i", r=PACK, i=4), in_=wa_raw[:].rearrange("p (c i r) -> p c r i", r=PACK, i=4))

        def deal_wb():
            nc.vector.tensor_copy(out=wb[:].rearrange("p (r m e) -> p r m e", r=PACK, e=2), in_=wb_raw[:].rearrange("p (m r e) -> p r m e", r=PACK, e=2))

        def deal_scales():
            nc.vector.tensor_copy(out=ws[:].rearrange("p (r m) -> p r m", r=PACK), in_=ws_raw[:].rearrange("p (m r) -> p r m", r=PACK))

        def multiply(o, z, h):
            cols = slice(h * HALF, (h + 1) * HALF) if o == "a" else slice(0, T)
            for r in range(PACK):
                c0 = (r * PASSES + z) * P
                if o == "a":
                    lhs, lhs_scale, fmt = wa[:, c0 : c0 + P].bitcast(E4M3), ws[WA_ROW:P, c0 : c0 + P], E4M3
                else:
                    lhs, lhs_scale, fmt = wb[:, 2 * c0 : 2 * c0 + 2 * P].bitcast(E2M1), ws[:, c0 : c0 + P], E5M2
                nc.tensor.matmul_mx(out=acc[h, r][:, cols], lhsT=lhs, lhsT_scale=lhs_scale, rhs=codes[o, z][:, cols].bitcast(fmt), rhs_scale=scales[o, z][:, cols], start=(o, z) == ("c", 0), stop=(o, z) == ("a", 1))

        out_rows = out_0.rearrange("(p r) t -> p r t", r=PACK)
        out_words = out_1.rearrange("z p c r -> p (z c r)").bitcast(I32)

        def drain(engine, r, h):
            cols = slice(h * HALF, (h + 1) * HALF)
            if engine == "vector":
                nc.vector.tensor_copy(out=y[h][:, r, :], in_=acc[h, r][:, cols])
            else:
                nc.scalar.copy(out=y[h][:, r, :], in_=acc[h, r][:, cols])

        def store(h, r0, r1):
            nc.sync.dma_start(out=out_rows[:, r0:r1, h * HALF : (h + 1) * HALF], in_=y[h][:, r0:r1, :])

        def group_result(engine, h, t0, t1):
            interleave(engine, y_grouped[h][:, PACK * t0 : PACK * t1], y[h][:, :, t0:t1])

        def quantize_result(h, engine):
            cols = slice(h * HALF, (h + 1) * HALF)
            nc.vector.quantize_mx(out=y_codes[h][:].bitcast(E4M3), scales=y_scales[:, cols], in_=y_grouped[h][:])
            engine.dma_start(out=out_words[:, cols], in_=y_codes[h][:])

        A, B = (0, HALF), (HALF, T)
        clamp(0, 0, *A)
        clamp(0, 0, *B)
        cut(0, 0, 1, *A)
        cut(0, 0, 1, *B)
        clamp(0, 1)
        clamp(0, 2)
        cut(0, 1, 2)
        clamp(0, 3)
        cut(0, 2, 3)
        cut(0, 3, 4)
        for o, j in (("a", 0), ("c", 0), ("a", 1), ("a", 2), ("c", 1), ("c", 2), ("c", 3)):
            scale_row("scalar", o, 0, j)
        for j in range(PACK):
            clamp(1, j, *A)
        deal_wb()
        scale_row("scalar", "a", 0, 3)
        group("scalar", "c", 0, *B)
        group("vector", "c", 0, *A)
        deal_scales()
        quantize("c", 0)
        multiply("c", 0, 0)
        multiply("c", 0, 1)
        cut(1, 0, 4, *A)
        group("scalar", "a", 0)
        deal_wa()
        for j in range(PACK):
            scale_row("vector", "c", 1, j, *A)
        for j in range(PACK):
            scale_row("scalar", "a", 1, j, *A)
        group("scalar", "c", 1, *A)
        for j in range(PACK):
            clamp(1, j, *B)
        quantize("a", 0)
        multiply("a", 0, 0)
        multiply("a", 0, 1)
        group("scalar", "a", 1, *A)
        cut(1, 0, 4, *B)
        quantize("c", 1, *A)
        multiply("c", 1, 0)
        for j in range(PACK):
            scale_row("vector", "c", 1, j, *B)
        for j in range(PACK):
            scale_row("scalar", "a", 1, j, *B)
        quantize("a", 1, *A)
        multiply("a", 1, 0)
        group("vector", "c", 1, *B)
        drain("vector", 0, 0)
        quantize("c", 1, *B)
        multiply("c", 1, 1)
        group("vector", "a", 1, *B)
        drain("scalar", 1, 0)
        store(0, 0, 2)
        drain("scalar", 2, 0)
        drain("scalar", 3, 0)
        store(0, 2, 4)
        group_result("vector", 0, 0, LAST_SPLIT)
        group_result("scalar", 0, LAST_SPLIT, HALF)
        quantize("a", 1, *B)
        multiply("a", 1, 1)
        quantize_result(0, nc.sync)
        for r in range(PACK):
            drain("vector" if r % 2 == 0 else "scalar", r, 1)
            if r % 2 == 1:
                store(1, r - 1, r + 1)
        group_result("vector", 1, 0, LAST_SPLIT)
        group_result("scalar", 1, LAST_SPLIT, HALF)
        quantize_result(1, nc.scalar)
        ys_words = y_scales[:].bitcast(I32)
        out_scales = out_2[0].bitcast(I32)
        for q in range(4):
            engine = nc.scalar if q == 3 else nc.sync
            engine.dma_start(out=out_scales[4 * q : 4 * q + 4, :], in_=ys_words[32 * q : 32 * q + 4, :])
